import numpy as np
import ml_dtypes


def mxq(x, axis, fmt="e4m3"):
    dtype, down = {"e4m3": (ml_dtypes.float8_e4m3fn, 7), "e5m2": (ml_dtypes.float8_e5m2, 14)}[fmt]
    v = np.moveaxis(np.asarray(x, np.float32).astype(ml_dtypes.bfloat16).astype(np.float64), axis, -1)
    blocks = v.reshape(v.shape[:-1] + (-1, 32))
    amax = np.abs(blocks).max(-1, keepdims=True)
    byte = np.maximum(np.where(amax > 0, np.frexp(amax)[1] - 1 + 127, 0) - down, 1)
    scale = np.exp2(byte - 127.0)
    codes = (blocks / scale).astype(np.float32).astype(dtype).astype(np.float64)
    return np.moveaxis((codes * scale).reshape(v.shape), -1, axis)


WIDE = False


def mx_kscale(k):
    if not WIDE:
        return np.ones(k)
    levels = np.array([30, -30])
    if k % 512:
        return np.exp2(np.random.permutation(np.resize(levels, k // 32))).repeat(32)
    a = np.empty((k // 512, 16))
    for p in range(k // 512):
        a[p, :8] = np.random.permutation(np.resize(levels, 8))
        for g in range(8):
            far = levels[np.abs(levels - a[p, g]) >= 10]
            a[p, g + 8] = far[np.random.randint(len(far))]
    return np.exp2(a.ravel()).repeat(32)


BF16 = ml_dtypes.bfloat16


def bf(x):
    return np.asarray(x, np.float32).astype(BF16)


def f64(x):
    return np.asarray(x).astype(np.float64)


E2M1 = np.array([0.0, 0.5, 1.0, 1.5, 2.0, 3.0, 4.0, 6.0, -0.0, -0.5, -1.0, -1.5, -2.0, -3.0, -4.0, -6.0])


def pack_weight(w, fmt):
    k, n = w.shape
    w = f64(bf(w)).reshape(k // 32, 32, n)
    amax = np.abs(w).max(1)
    if fmt == "e4m3":
        byte = np.frexp(amax)[1] - 1 + 127 - 7
    else:
        mant, ex = np.frexp(amax / 6.0)
        byte = np.where(mant > 0.5, ex, ex - 1) + 127
    byte = np.clip(np.where(amax > 0, byte, 1), 1, 254)
    scaled = (w * np.exp2(127.0 - byte)[:, None, :]).reshape(k, n).astype(np.float32)
    by_word = np.ascontiguousarray(scaled.reshape(k // 512, 128, 4, n).transpose(0, 1, 3, 2))
    if fmt == "e4m3":
        words = by_word.astype(ml_dtypes.float8_e4m3fn).view(np.uint8)
    else:
        c = by_word.astype(ml_dtypes.float4_e2m1fn).view(np.uint8) & 0xF
        words = c[..., 0::2] | (c[..., 1::2] << 4)
    return np.ascontiguousarray(words), np.ascontiguousarray(byte.astype(np.uint8).reshape(k // 512, 16, n))


def unpack_weight(words, scales, fmt):
    g, p, n, _ = words.shape
    if fmt == "e4m3":
        vals = np.ascontiguousarray(words).view(ml_dtypes.float8_e4m3fn).astype(np.float64)
    else:
        nib = np.empty((g, p, n, 4), np.uint8)
        nib[..., 0::2] = words & 0xF
        nib[..., 1::2] = words >> 4
        vals = E2M1[nib]
    vals = vals * np.repeat(np.exp2(scales.astype(np.float64) - 127.0), 8, axis=1)[..., None]
    return vals.transpose(0, 1, 3, 2).reshape(g * 512, n)
def pack4(w):
    words, scales = pack_weight(w, "e2m1")
    return words.reshape(words.shape[0], 128, -1), scales


def unpack4(words, scales):
    return unpack_weight(words.reshape(words.shape[0], 128, -1, 2), scales, "e2m1")


M, K, C, D = 2048, 1024, 512, 1024
WIDTH = 0.7


def setup_inputs():
    s = mx_kscale(K)
    t = mx_kscale(M)
    x = np.random.standard_normal((M, K)) * s
    w = WIDTH * np.random.standard_normal((K, C)) / np.sqrt(K) / s[:, None]
    w_words, w_scales = pack4(w)
    b = 0.3 * np.random.standard_normal(C)
    m = np.random.uniform(0.5, 1.5, M) / np.sqrt(M) * t
    v = np.random.standard_normal((M, D)) / t[:, None]
    r = 1 + 0.1 * np.random.standard_normal(C)
    return {"x": bf(x), "w_words": w_words, "w_scales": w_scales,
            "b": bf(b), "m": bf(m), "v": bf(v), "r": bf(r)}


def reference(x, w_words, w_scales, b, m, v, r):
    w = unpack4(w_words, w_scales)
    z = mxq(f64(x), 1, "e4m3") @ w
    scores = np.exp(z + f64(b))
    a = scores * f64(m)[:, None]
    sums = mxq(a, 0, "e5m2").T @ mxq(f64(v), 0, "e4m3")
    centres = sums * f64(r)[:, None]
    return scores, centres

@@ -1,0 +1,277 @@
+from contextlib import ExitStack
+
+import concourse.mybir as mybir
+from concourse.masks import make_identity
+
+M, K, C, D = 2048, 1024, 512, 1024
+FLOPS = 2 * M * K * C + 2 * M * C * D
+
+F32 = mybir.dt.float32
+BF16 = mybir.dt.bfloat16
+I32 = mybir.dt.int32
+U32 = mybir.dt.uint32
+U8 = mybir.dt.uint8
+E4M3 = mybir.dt.float8_e4m3fn_x4
+E5M2 = mybir.dt.float8_e5m2_x4
+E2M1 = mybir.dt.float4_e2m1fn_x4
+ACT = mybir.ActivationFunctionType
+ALU = mybir.AluOpType
+
+P = 128
+PACK = 4
+GROUP = P * PACK
+GROUPS = M // GROUP
+K_PASSES = K // GROUP
+CHUNKS = C // P
+BANK = 512
+HALVES = D // BANK
+PIECE = 256
+PIECES = D // PIECE
+TILES = GROUPS * PACK
+LAST = GROUPS - 1
+
+
+def tile_scaled_cluster_sums_s9_kernel(tc, x, w_words, w_scales, b, m, v, r, out_0, out_1):
+    nc = tc.nc
+    x_rows = x.rearrange("(g p t) k -> g p t k", p=P, t=PACK)
+    v_rows = v.rearrange("(g p t) d -> g p t d", p=P, t=PACK)
+    score_rows = out_0.rearrange("(g p t) c -> g p t c", p=P, t=PACK)
+
+    with ExitStack() as ctx:
+        keep = ctx.enter_context(tc.tile_pool(name="keep", bufs=1))
+        work = ctx.enter_context(tc.tile_pool(name="work", bufs=3))
+        psum = ctx.enter_context(tc.psum_pool(name="psum", bufs=1))
+        ctx.enter_context(tc.manual_schedule())
+
+        ident = keep.tile([P, P], F32, name="ident")
+        make_identity(nc, ident[:])
+        w_plane = keep.tile([P, K_PASSES, C], U8, name="w_plane", align_bytes=64)
+        nc.vector.memset(w_plane[:].rearrange("p h c -> p (h c)").bitcast(I32), 0)
+
+        x_sb, v_sb = {}, {}
+
+        def load_x(g, t0, count):
+            rows = keep.tile([P, count, K], BF16, name="x_%d_%d" % (g, t0))
+            nc.sync.dma_start(out=rows[:], in_=x_rows[g, :, t0 : t0 + count, :])
+            for t in range(count):
+                x_sb[PACK * g + t0 + t] = rows[:, t, :]
+
+        def load_v(g, q0, count):
+            cols = keep.tile([P, PACK, count * PIECE], BF16, name="v_%d_%d" % (g, q0))
+            nc.sync.dma_start(out=cols[:], in_=v_rows[g, :, :, q0 * PIECE : (q0 + count) * PIECE])
+            for q in range(count):
+                v_sb[PIECES * g + q0 + q] = cols[:, :, q * PIECE : (q + 1) * PIECE]
+
+        b_cols = keep.tile([P, PACK], BF16, name="b_cols")
+        nc.sync.dma_start(out=b_cols[:], in_=b.rearrange("(p j) -> p j", j=PACK))
+        load_x(0, 0, 1)
+        load_v(0, 0, 1)
+        load_x(0, 1, 1)
+        w_codes = keep.tile([P, K_PASSES, 2 * C], U8, name="w_codes", align_bytes=64)
+        nc.sync.dma_start(out=w_codes[:].bitcast(I32), in_=w_words.rearrange("h p n -> p h n").bitcast(I32))
+        for quad in range(4):
+            nc.sync.dma_start(
+                out=w_plane[32 * quad : 32 * quad + 4, :, :].bitcast(I32),
+                in_=w_scales[:, 4 * quad : 4 * quad + 4, :].rearrange("h q c -> q h c").bitcast(I32),
+            )
+        load_v(0, 1, 1)
+        load_x(0, 2, 2)
+        load_v(0, 2, 2)
+        load_x(1, 0, 2)
+        load_v(1, 0, 2)
+        load_x(1, 2, 2)
+        load_v(1, 2, 2)
+        m_cols = keep.tile([P, GROUPS, PACK], BF16, name="m_cols")
+        nc.sync.dma_start(out=m_cols[:], in_=m.rearrange("(g p t) -> p g t", p=P, t=PACK))
+        for g in range(2, GROUPS):
+            load_x(g, 0, PACK)
+            load_v(g, 0, PIECES)
+        r_cols = keep.tile([P, CHUNKS, 2], BF16, name="r_cols")
+        with nc.allow_non_contiguous_dma(reason="one factor to a partition"):
+            nc.sync.dma_start(out=r_cols[:, :, 0], in_=r.rearrange("(j p) -> p j", p=P))
+
+        xt_bank, xt_sb, x_codes, x_plane = {}, {}, {}, {}
+        z_bank, zb_sb, a_sb, a_codes, a_plane = {}, {}, {}, {}, {}
+        vi_sb, v_codes, v_plane, acc, cen = {}, {}, {}, {}, {}
+        scores = [keep.tile([P, PACK, C], F32, name="scores_%d" % g) for g in range(GROUPS)]
+        for g in range(GROUPS):
+            for h in range(HALVES):
+                v_codes[g, h] = keep.tile([P, BANK], U32, name="v_codes_%d_%d" % (g, h), align_bytes=64)
+                v_plane[g, h] = keep.tile([P, BANK], U8, name="v_plane_%d_%d" % (g, h), align_bytes=64)
+
+        def transpose_x(u):
+            words = x_sb[u].bitcast(F32)
+            xt_bank[u] = psum.tile([P, K_PASSES, 2, P], F32, name="xt_bank", tag="xt", bufs=2)
+            for h in range(K_PASSES):
+                for e in range(2):
+                    nc.tensor.transpose(xt_bank[u][:, h, e, :], words[:, 256 * h + e : 256 * (h + 1) : 2], ident[:])
+
+        def copy_x(u):
+            xt_sb[u] = work.tile([P, K_PASSES * P * PACK], BF16, name="xt_sb", align_bytes=64)
+            nc.scalar.copy(
+                out=xt_sb[u][:].bitcast(F32).rearrange("p (h s e) -> p h s e", h=K_PASSES, e=2),
+                in_=xt_bank[u][:].rearrange("p h e s -> p h s e"),
+            )
+
+        def quantize_x(u):
+            x_codes[u] = keep.tile([P, K_PASSES * P], U32, name="x_codes_%d" % u, align_bytes=64)
+            x_plane[u] = keep.tile([P, K_PASSES * P], U8, name="x_plane_%d" % u, align_bytes=64)
+            nc.vector.quantize_mx(out=x_codes[u][:].bitcast(E4M3), scales=x_plane[u][:], in_=xt_sb[u][:])
+
+        def logits(u):
+            z_bank[u] = psum.tile([P, BANK], F32, name="z_bank", tag="z", bufs=2)
+            for h in range(K_PASSES):
+                nc.tensor.matmul_mx(
+                    out=z_bank[u][:],
+                    lhsT=x_codes[u][:, h * P : (h + 1) * P].bitcast(E4M3),
+                    lhsT_scale=x_plane[u][:, h * P : (h + 1) * P],
+                    rhs=w_codes[:, h, :].bitcast(E2M1),
+                    rhs_scale=w_plane[:, h, :],
+                    start=(h == 0),
+                    stop=(h == K_PASSES - 1),
+                )
+
+        def add_bias(u):
+            zb_sb[u] = work.tile([P, BANK], F32, name="zb_sb")
+            nc.vector.tensor_tensor(out=zb_sb[u][:], in0=z_bank[u][:], in1=bias[:], op=ALU.add)
+
+        def exp_scores(u):
+            g, t = divmod(u, PACK)
+            nc.scalar.activation(out=scores[g][:, t, :], in_=zb_sb[u][:], func=ACT.Exp)
+            if t % 2 == 1:
+                nc.sync.dma_start(out=score_rows[g, :, t - 1 : t + 1, :], in_=scores[g][:, t - 1 : t + 1, :])
+
+        def weigh(n):
+            g, j = divmod(n, CHUNKS)
+            a_sb[n] = work.tile([P, P * PACK], BF16, name="a_sb", align_bytes=64)
+            nc.vector.tensor_tensor(
+                out=a_sb[n][:].rearrange("p (c i t) -> p c t i", i=4, t=PACK),
+                in0=scores[g][:, :, j * P : (j + 1) * P].rearrange("p t (c i) -> p c t i", i=4),
+                in1=m_cols[:, g, :].unsqueeze(1).unsqueeze(3).broadcast_to([P, P // 4, PACK, 4]),
+                op=ALU.mult,
+            )
+
+        def quantize_a(n):
+            a_codes[n] = keep.tile([P, P], U32, name="a_codes_%d" % n, align_bytes=64)
+            a_plane[n] = keep.tile([P, P], U8, name="a_plane_%d" % n, align_bytes=64)
+            nc.vector.quantize_mx(out=a_codes[n][:].bitcast(E5M2), scales=a_plane[n][:], in_=a_sb[n][:])
+
+        def interleave_v(k, copy, c0, width):
+            if c0 == 0:
+                vi_sb[k] = work.tile([P, PIECE * PACK], BF16, name="vi_sb", align_bytes=64, bufs=6)
+            copy(
+                out=vi_sb[k][:, c0 * PACK : (c0 + width) * PACK].rearrange("p (c i t) -> p c t i", i=4, t=PACK),
+                in_=v_sb[k][:, :, c0 : c0 + width].rearrange("p t (c i) -> p c t i", i=4),
+            )
+
+        def quantize_v(k):
+            g, q = divmod(k, PIECES)
+            h, cols = q // 2, slice((q % 2) * PIECE, (q % 2 + 1) * PIECE)
+            nc.vector.quantize_mx(out=v_codes[g, h][:, cols].bitcast(E4M3), scales=v_plane[g, h][:, cols], in_=vi_sb[k][:])
+
+        def sums(g, j, h):
+            if g == 0:
+                tag = ["acc_0_%d" % h, "acc_1_%d" % h, "xt", "z"][j]
+                acc[j, h] = psum.tile([P, BANK], F32, name="acc", tag=tag, bufs=1 if j < 2 else 2)
+            n = CHUNKS * g + j
+            nc.tensor.matmul_mx(
+                out=acc[j, h][:],
+                lhsT=a_codes[n][:].bitcast(E5M2),
+                lhsT_scale=a_plane[n][:],
+                rhs=v_codes[g, h][:].bitcast(E4M3),
+                rhs_scale=v_plane[g, h][:],
+                start=(g == 0),
+                stop=(g == LAST),
+            )
+
+        def centres(j, h, on_vector):
+            if h == 0:
+                cen[j] = keep.tile([P, D], F32, name="cen_%d" % j)
+            cols = slice(h * BANK, (h + 1) * BANK)
+            if on_vector:
+                nc.vector.tensor_scalar(out=cen[j][:, cols], in0=acc[j, h][:], scalar1=r_f32[:, j : j + 1], scalar2=None, op0=ALU.mult)
+            else:
+                nc.scalar.activation(out=cen[j][:, cols], in_=acc[j, h][:], func=ACT.Copy, scale=r_f32[:, j : j + 1])
+            if j == CHUNKS - 1:
+                nc.sync.dma_start(out=out_1[j * P : (j + 1) * P, cols], in_=cen[j][:, cols])
+            elif h == HALVES - 1:
+                nc.sync.dma_start(out=out_1[j * P : (j + 1) * P, :], in_=cen[j][:])
+
+        b_f32 = keep.tile([P, PACK], F32, name="b_f32")
+        nc.scalar.activation(out=b_f32[:], in_=b_cols[:], func=ACT.Copy)
+        transpose_x(0)
+        bias_bank = psum.tile([P, PACK, P], F32, name="bias_bank", tag="acc_0_0", bufs=1)
+        for j in range(PACK):
+            nc.tensor.transpose(bias_bank[:, j, :], b_f32[:, j : j + 1].to_broadcast([P, P]), ident[:])
+        transpose_x(1)
+        copy_x(0)
+        bias = keep.tile([P, C], F32, name="bias")
+        nc.scalar.copy(out=bias[:].rearrange("p (n j) -> p n j", j=PACK), in_=bias_bank[:].rearrange("p j n -> p n j"))
+        interleave_v(0, nc.vector.tensor_copy, 0, PIECE)
+        quantize_v(0)
+        r_f32 = keep.tile([P, CHUNKS], F32, name="r_f32")
+
+        weigh_at = {PACK * g + 5 + j: CHUNKS * g + j for g in range(LAST) for j in range(3)}
+        vector_v_at = {0: [1], 1: [2], 2: [3], 3: [4], 4: [6], 8: [9], 12: [12]}
+        scalar_v = [5, 7, 8, 10, 11, 13, 14, 15]
+        scalar_at = {14: [12, 13], 15: [14, 15]}
+        for s in range(2, TILES - 2):
+            scalar_at[s] = [s - 2]
+        sums_at = {7: [(0, 0, 0)], 8: [(0, 0, 1)], 9: [(0, 1, 0)], 10: [(0, 1, 1)],
+                   11: [(1, 0, 0)], 12: [(1, 0, 1)], 13: [(1, 1, 0), (1, 1, 1)],
+                   14: [(2, 0, 0), (2, 0, 1), (0, 2, 0), (1, 2, 0)],
+                   15: [(2, 1, 0), (2, 1, 1), (0, 2, 1), (1, 2, 1)]}
+        weighed, interleaved = None, []
+        for s in range(TILES):
+            if s + 1 < TILES:
+                copy_x(s + 1)
+            quantize_x(s)
+            logits(s)
+            if s + 2 < TILES:
+                transpose_x(s + 2)
+            if s >= 1:
+                add_bias(s - 1)
+            if weighed is not None:
+                quantize_a(weighed)
+            weighed = weigh_at.get(s)
+            if weighed is not None:
+                weigh(weighed)
+            for k in vector_v_at.get(s, []):
+                interleave_v(k, nc.vector.tensor_copy, 0, PIECE)
+            for k in interleaved:
+                quantize_v(k)
+            interleaved = list(vector_v_at.get(s, []))
+            for n in scalar_at.get(s, []):
+                i, half = divmod(n, 2)
+                interleave_v(scalar_v[i], nc.scalar.copy, half * PIECE // 2, PIECE // 2)
+                if half == 1:
+                    interleaved.append(scalar_v[i])
+            if s >= 1:
+                exp_scores(s - 1)
+            for g, j, h in sums_at.get(s, []):
+                sums(g, j, h)
+
+        nc.scalar.copy(out=r_f32[:], in_=r_cols[:, :, 0])
+        add_bias(TILES - 1)
+        exp_scores(TILES - 1)
+        quantize_a(weighed)
+        for h in range(HALVES):
+            sums(LAST - 1, 2, h)
+        for k in interleaved:
+            quantize_v(k)
+        order = [(0, 3), (LAST, 0), (LAST, 1), (LAST, 2), (1, 3), (2, 3), (LAST, 3)]
+        for i, (g, j) in enumerate(order):
+            weigh(CHUNKS * g + j)
+            if i >= 1:
+                gp, jp = order[i - 1]
+                quantize_a(CHUNKS * gp + jp)
+                for h in range(HALVES):
+                    sums(gp, jp, h)
+                if gp == LAST:
+                    for h in range(HALVES):
+                        centres(jp, h, False)
+        quantize_a(TILES - 1)
+        for h in range(HALVES):
+            sums(LAST, 3, h)
+        centres(3, 0, False)
+        centres(3, 1, True)

@@ -45,6 +45,8 @@ def tile_scaled_cluster_sums_s9_kernel(tc, x, w_words, w_scales, b, m, v, r, out
 
         ident = keep.tile([P, P], F32, name="ident")
         make_identity(nc, ident[:])
+        rows_mr = keep.tile([P, GROUP + P], BF16, name="rows_mr")
+        nc.gpsimd.memset(rows_mr[:].bitcast(I32), 0)
         w_plane = keep.tile([P, K_PASSES, C], U8, name="w_plane", align_bytes=64)
         nc.vector.memset(w_plane[:].rearrange("p h c -> p (h c)").bitcast(I32), 0)
 
@@ -76,19 +78,17 @@ def tile_scaled_cluster_sums_s9_kernel(tc, x, w_words, w_scales, b, m, v, r, out
             )
         load_v(0, 1, 1)
         load_x(0, 2, 2)
-        load_v(0, 2, 2)
         load_x(1, 0, 2)
-        load_v(1, 0, 2)
+        load_v(0, 2, 2)
         load_x(1, 2, 2)
+        nc.sync.dma_start(out=rows_mr[0:GROUPS, 0:GROUP], in_=m.rearrange("(g s) -> g s", g=GROUPS))
+        nc.sync.dma_start(out=rows_mr[0:CHUNKS, GROUP : GROUP + P], in_=r.rearrange("(j c) -> j c", j=CHUNKS))
+        load_v(1, 0, 2)
+        load_x(2, 0, 4)
         load_v(1, 2, 2)
-        m_cols = keep.tile([P, GROUPS, PACK], BF16, name="m_cols")
-        nc.sync.dma_start(out=m_cols[:], in_=m.rearrange("(g p t) -> p g t", p=P, t=PACK))
-        for g in range(2, GROUPS):
-            load_x(g, 0, PACK)
-            load_v(g, 0, PIECES)
-        r_cols = keep.tile([P, CHUNKS, 2], BF16, name="r_cols")
-        with nc.allow_non_contiguous_dma(reason="one factor to a partition"):
-            nc.sync.dma_start(out=r_cols[:, :, 0], in_=r.rearrange("(j p) -> p j", p=P))
+        load_v(2, 0, 4)
+        load_x(3, 0, 4)
+        load_v(3, 0, 4)
 
         xt_bank, xt_sb, x_codes, x_plane = {}, {}, {}, {}
         z_bank, zb_sb, a_sb, a_codes, a_plane = {}, {}, {}, {}, {}
@@ -101,7 +101,10 @@ def tile_scaled_cluster_sums_s9_kernel(tc, x, w_words, w_scales, b, m, v, r, out
 
         def transpose_x(u):
             words = x_sb[u].bitcast(F32)
-            xt_bank[u] = psum.tile([P, K_PASSES, 2, P], F32, name="xt_bank", tag="xt", bufs=2)
+            if u in (2, 5):
+                xt_bank[u] = psum.tile([P, K_PASSES, 2, P], F32, name="xt_bank", tag="acc_1_0", bufs=1)
+            else:
+                xt_bank[u] = psum.tile([P, K_PASSES, 2, P], F32, name="xt_bank", tag="xt", bufs=2)
             for h in range(K_PASSES):
                 for e in range(2):
                     nc.tensor.transpose(xt_bank[u][:, h, e, :], words[:, 256 * h + e : 256 * (h + 1) : 2], ident[:])
@@ -131,6 +134,16 @@ def tile_scaled_cluster_sums_s9_kernel(tc, x, w_words, w_scales, b, m, v, r, out
                     stop=(h == K_PASSES - 1),
                 )
 
+        def turn_m_and_r():
+            r_rows = keep.tile([P, P], F32, name="r_rows")
+            nc.scalar.activation(out=r_rows[:], in_=rows_mr[:, GROUP : GROUP + P], func=ACT.Copy)
+            m_words = rows_mr[:, 0:GROUP].bitcast(F32)
+            bank = psum.tile([P, 3, P], F32, name="mr_bank", tag="acc_0_1", bufs=1)
+            for e in range(2):
+                nc.tensor.transpose(bank[:, e, :], m_words[:, e : 2 * P : 2], ident[:])
+            nc.tensor.transpose(bank[:, 2, :], r_rows[:], ident[:])
+            return bank
+
         def add_bias(u):
             zb_sb[u] = work.tile([P, BANK], F32, name="zb_sb")
             nc.vector.tensor_tensor(out=zb_sb[u][:], in0=z_bank[u][:], in1=bias[:], op=ALU.add)
@@ -145,9 +158,9 @@ def tile_scaled_cluster_sums_s9_kernel(tc, x, w_words, w_scales, b, m, v, r, out
             g, j = divmod(n, CHUNKS)
             a_sb[n] = work.tile([P, P * PACK], BF16, name="a_sb", align_bytes=64)
             nc.vector.tensor_tensor(
-                out=a_sb[n][:].rearrange("p (c i t) -> p c t i", i=4, t=PACK),
-                in0=scores[g][:, :, j * P : (j + 1) * P].rearrange("p t (c i) -> p c t i", i=4),
-                in1=m_cols[:, g, :].unsqueeze(1).unsqueeze(3).broadcast_to([P, P // 4, PACK, 4]),
+                out=a_sb[n][:].rearrange("p (c i t) -> p c t i", i=2, t=PACK),
+                in0=scores[g][:, :, j * P : (j + 1) * P].rearrange("p t (c i) -> p c t i", i=2),
+                in1=m_cols[:, g, :].unsqueeze(1).unsqueeze(3).broadcast_to([P, P // 2, PACK, 2]),
                 op=ALU.mult,
             )
 
@@ -184,18 +197,17 @@ def tile_scaled_cluster_sums_s9_kernel(tc, x, w_words, w_scales, b, m, v, r, out
                 stop=(g == LAST),
             )
 
-        def centres(j, h, on_vector):
-            if h == 0:
-                cen[j] = keep.tile([P, D], F32, name="cen_%d" % j)
-            cols = slice(h * BANK, (h + 1) * BANK)
-            if on_vector:
-                nc.vector.tensor_scalar(out=cen[j][:, cols], in0=acc[j, h][:], scalar1=r_f32[:, j : j + 1], scalar2=None, op0=ALU.mult)
-            else:
-                nc.scalar.activation(out=cen[j][:, cols], in_=acc[j, h][:], func=ACT.Copy, scale=r_f32[:, j : j + 1])
-            if j == CHUNKS - 1:
-                nc.sync.dma_start(out=out_1[j * P : (j + 1) * P, cols], in_=cen[j][:, cols])
-            elif h == HALVES - 1:
-                nc.sync.dma_start(out=out_1[j * P : (j + 1) * P, :], in_=cen[j][:])
+        def centres(j, h, on_vector, parts=1):
+            width = BANK // parts
+            for i in range(parts):
+                cen = keep.tile([P, width], F32, name="cen_%d_%d_%d" % (j, h, i))
+                src = acc[j, h][:, i * width : (i + 1) * width]
+                if on_vector:
+                    nc.vector.tensor_scalar(out=cen[:], in0=src, scalar1=r_f32[:, j : j + 1], scalar2=None, op0=ALU.mult)
+                else:
+                    nc.scalar.activation(out=cen[:], in_=src, func=ACT.Copy, scale=r_f32[:, j : j + 1])
+                d0 = h * BANK + i * width
+                nc.sync.dma_start(out=out_1[j * P : (j + 1) * P, d0 : d0 + width], in_=cen[:])
 
         b_f32 = keep.tile([P, PACK], F32, name="b_f32")
         nc.scalar.activation(out=b_f32[:], in_=b_cols[:], func=ACT.Copy)
@@ -210,25 +222,36 @@ def tile_scaled_cluster_sums_s9_kernel(tc, x, w_words, w_scales, b, m, v, r, out
         interleave_v(0, nc.vector.tensor_copy, 0, PIECE)
         quantize_v(0)
         r_f32 = keep.tile([P, CHUNKS], F32, name="r_f32")
+        m_cols = keep.tile([P, GROUPS, PACK], BF16, name="m_cols")
 
         weigh_at = {PACK * g + 5 + j: CHUNKS * g + j for g in range(LAST) for j in range(3)}
-        vector_v_at = {0: [1], 1: [2], 2: [3], 3: [4], 4: [6], 8: [9], 12: [12]}
-        scalar_v = [5, 7, 8, 10, 11, 13, 14, 15]
-        scalar_at = {14: [12, 13], 15: [14, 15]}
-        for s in range(2, TILES - 2):
-            scalar_at[s] = [s - 2]
-        sums_at = {7: [(0, 0, 0)], 8: [(0, 0, 1)], 9: [(0, 1, 0)], 10: [(0, 1, 1)],
-                   11: [(1, 0, 0)], 12: [(1, 0, 1)], 13: [(1, 1, 0), (1, 1, 1)],
-                   14: [(2, 0, 0), (2, 0, 1), (0, 2, 0), (1, 2, 0)],
-                   15: [(2, 1, 0), (2, 1, 1), (0, 2, 1), (1, 2, 1)]}
+        vector_v_at = {0: [1], 2: [2], 3: [3], 4: [4], 8: [8], 12: [11]}
+        scalar_v = [5, 6, 7, 9, 10, 12, 13]
+        scalar_at = {14: [10, 11], 15: [12, 13]}
+        for s in range(4, TILES - 2):
+            scalar_at[s] = [s - 4]
+        sums_at = {6: [(0, 0, 0)], 7: [(0, 0, 1)], 8: [(0, 1, 0)], 9: [(0, 1, 1)],
+                   10: [(1, 0, 0)], 11: [(1, 0, 1)], 12: [(1, 1, 0)], 13: [(1, 1, 1), (0, 2, 0), (1, 2, 0)],
+                   14: [(2, 0, 0), (0, 2, 1), (1, 2, 1), (2, 0, 1)],
+                   15: [(2, 1, 0), (2, 1, 1)]}
         weighed, interleaved = None, []
         for s in range(TILES):
             if s + 1 < TILES:
                 copy_x(s + 1)
             quantize_x(s)
             logits(s)
-            if s + 2 < TILES:
+            if s == 0:
+                transpose_x(2)
+            if s < 5:
+                transpose_x(s + 3)
+            elif s > 5 and s + 2 < TILES:
                 transpose_x(s + 2)
+            if s == 3:
+                mr_bank = turn_m_and_r()
+            if s == 4:
+                nc.scalar.copy(out=m_cols[:].rearrange("p g t -> p (g t)").bitcast(F32).rearrange("p (g e) -> p g e", e=2),
+                               in_=mr_bank[:, 0:2, 0:GROUPS].rearrange("p e g -> p g e"))
+                nc.scalar.copy(out=r_f32[:], in_=mr_bank[:, 2, 0:CHUNKS])
             if s >= 1:
                 add_bias(s - 1)
             if weighed is not None:
@@ -251,27 +274,46 @@ def tile_scaled_cluster_sums_s9_kernel(tc, x, w_words, w_scales, b, m, v, r, out
             for g, j, h in sums_at.get(s, []):
                 sums(g, j, h)
 
-        nc.scalar.copy(out=r_f32[:], in_=r_cols[:, :, 0])
         add_bias(TILES - 1)
         exp_scores(TILES - 1)
+        interleave_v(14, nc.scalar.copy, 0, PIECE)
+        interleave_v(15, nc.scalar.copy, 0, PIECE)
         quantize_a(weighed)
         for h in range(HALVES):
             sums(LAST - 1, 2, h)
         for k in interleaved:
             quantize_v(k)
-        order = [(0, 3), (LAST, 0), (LAST, 1), (LAST, 2), (1, 3), (2, 3), (LAST, 3)]
-        for i, (g, j) in enumerate(order):
-            weigh(CHUNKS * g + j)
-            if i >= 1:
-                gp, jp = order[i - 1]
-                quantize_a(CHUNKS * gp + jp)
-                for h in range(HALVES):
-                    sums(gp, jp, h)
-                if gp == LAST:
-                    for h in range(HALVES):
-                        centres(jp, h, False)
-        quantize_a(TILES - 1)
+        weigh(3)
+        weigh(12)
+        quantize_a(3)
+        sums(0, 3, 0)
+        sums(0, 3, 1)
+        weigh(13)
+        quantize_a(12)
+        sums(3, 0, 0)
+        weigh(14)
+        quantize_a(13)
+        sums(3, 1, 0)
+        quantize_v(14)
+        quantize_a(14)
+        sums(3, 2, 0)
+        quantize_v(15)
+        for j in range(3):
+            sums(3, j, 1)
         for h in range(HALVES):
-            sums(LAST, 3, h)
-        centres(3, 0, False)
-        centres(3, 1, True)
+            for j in range(3):
+                centres(j, h, False)
+        weigh(7)
+        weigh(11)
+        quantize_a(7)
+        sums(1, 3, 0)
+        sums(1, 3, 1)
+        weigh(15)
+        quantize_a(11)
+        sums(2, 3, 0)
+        quantize_a(15)
+        sums(3, 3, 0)
+        sums(2, 3, 1)
+        sums(3, 3, 1)
+        centres(3, 0, True, 2)
+        centres(3, 1, False, 2)

@@ -19,16 +19,17 @@ ALU = mybir.AluOpType
 
 P = 128
 PACK = 4
-GROUP = P * PACK
-GROUPS = M // GROUP
-K_PASSES = K // GROUP
+PASS = P * PACK
+K_PASSES = K // PASS
+GROUPS = M // PASS
+TILES = GROUPS * PACK
 CHUNKS = C // P
 BANK = 512
 HALVES = D // BANK
-PIECE = 256
+PIECE = BANK // 2
 PIECES = D // PIECE
-TILES = GROUPS * PACK
-LAST = GROUPS - 1
+LAST_GROUP = GROUPS - 1
+LAST_CHUNK = CHUNKS - 1
 
 
 def tile_scaled_cluster_sums_s9_kernel(tc, x, w_words, w_scales, b, m, v, r, out_0, out_1):
@@ -45,30 +46,31 @@ def tile_scaled_cluster_sums_s9_kernel(tc, x, w_words, w_scales, b, m, v, r, out
 
         ident = keep.tile([P, P], F32, name="ident")
         make_identity(nc, ident[:])
-        rows_mr = keep.tile([P, GROUP + P], BF16, name="rows_mr")
-        nc.gpsimd.memset(rows_mr[:].bitcast(I32), 0)
+        mr_rows = keep.tile([P, PASS + P], BF16, name="mr_rows")
+        nc.gpsimd.memset(mr_rows[:].bitcast(I32), 0)
         w_plane = keep.tile([P, K_PASSES, C], U8, name="w_plane", align_bytes=64)
         nc.vector.memset(w_plane[:].rearrange("p h c -> p (h c)").bitcast(I32), 0)
 
         x_sb, v_sb = {}, {}
 
-        def load_x(g, t0, count):
-            rows = keep.tile([P, count, K], BF16, name="x_%d_%d" % (g, t0))
-            nc.sync.dma_start(out=rows[:], in_=x_rows[g, :, t0 : t0 + count, :])
-            for t in range(count):
-                x_sb[PACK * g + t0 + t] = rows[:, t, :]
+        def load_x(u, count):
+            g, t = divmod(u, PACK)
+            rows = keep.tile([P, count, K], BF16, name="x_%d" % u)
+            nc.sync.dma_start(out=rows[:], in_=x_rows[g, :, t : t + count, :])
+            for i in range(count):
+                x_sb[u + i] = rows[:, i, :]
 
-        def load_v(g, q0, count):
-            cols = keep.tile([P, PACK, count * PIECE], BF16, name="v_%d_%d" % (g, q0))
-            nc.sync.dma_start(out=cols[:], in_=v_rows[g, :, :, q0 * PIECE : (q0 + count) * PIECE])
-            for q in range(count):
-                v_sb[PIECES * g + q0 + q] = cols[:, :, q * PIECE : (q + 1) * PIECE]
+        def load_v(k, count):
+            g, q = divmod(k, PIECES)
+            cols = keep.tile([P, PACK, count * PIECE], BF16, name="v_%d" % k)
+            nc.sync.dma_start(out=cols[:], in_=v_rows[g, :, :, q * PIECE : (q + count) * PIECE])
+            for i in range(count):
+                v_sb[k + i] = cols[:, :, i * PIECE : (i + 1) * PIECE]
 
         b_cols = keep.tile([P, PACK], BF16, name="b_cols")
         nc.sync.dma_start(out=b_cols[:], in_=b.rearrange("(p j) -> p j", j=PACK))
-        load_x(0, 0, 1)
-        load_v(0, 0, 1)
-        load_x(0, 1, 1)
+        load_x(0, 1)
+        load_x(1, 2)
         w_codes = keep.tile([P, K_PASSES, 2 * C], U8, name="w_codes", align_bytes=64)
         nc.sync.dma_start(out=w_codes[:].bitcast(I32), in_=w_words.rearrange("h p n -> p h n").bitcast(I32))
         for quad in range(4):
@@ -76,41 +78,64 @@ def tile_scaled_cluster_sums_s9_kernel(tc, x, w_words, w_scales, b, m, v, r, out
                 out=w_plane[32 * quad : 32 * quad + 4, :, :].bitcast(I32),
                 in_=w_scales[:, 4 * quad : 4 * quad + 4, :].rearrange("h q c -> q h c").bitcast(I32),
             )
-        load_v(0, 1, 1)
-        load_x(0, 2, 2)
-        load_x(1, 0, 2)
-        load_v(0, 2, 2)
-        load_x(1, 2, 2)
-        nc.sync.dma_start(out=rows_mr[0:GROUPS, 0:GROUP], in_=m.rearrange("(g s) -> g s", g=GROUPS))
-        nc.sync.dma_start(out=rows_mr[0:CHUNKS, GROUP : GROUP + P], in_=r.rearrange("(j c) -> j c", j=CHUNKS))
-        load_v(1, 0, 2)
-        load_x(2, 0, 4)
-        load_v(1, 2, 2)
-        load_v(2, 0, 4)
-        load_x(3, 0, 4)
-        load_v(3, 0, 4)
+        load_v(0, 2)
+        load_x(3, 1)
+        load_x(4, 2)
+        load_v(2, 2)
+        load_x(6, 2)
+        nc.sync.dma_start(out=mr_rows[0:GROUPS, 0:PASS], in_=m.rearrange("(g s) -> g s", g=GROUPS))
+        nc.sync.dma_start(out=mr_rows[0:CHUNKS, PASS : PASS + P], in_=r.rearrange("(j c) -> j c", j=CHUNKS))
+        load_v(4, 2)
+        load_x(8, PACK)
+        load_v(6, 2)
+        load_v(8, PIECES)
+        load_x(12, PACK)
+        load_v(12, PIECES)
 
         xt_bank, xt_sb, x_codes, x_plane = {}, {}, {}, {}
         z_bank, zb_sb, a_sb, a_codes, a_plane = {}, {}, {}, {}, {}
-        vi_sb, v_codes, v_plane, acc, cen = {}, {}, {}, {}, {}
+        vi_sb, v_codes, v_plane, acc = {}, {}, {}, {}
         scores = [keep.tile([P, PACK, C], F32, name="scores_%d" % g) for g in range(GROUPS)]
-        for g in range(GROUPS):
-            for h in range(HALVES):
-                v_codes[g, h] = keep.tile([P, BANK], U32, name="v_codes_%d_%d" % (g, h), align_bytes=64)
-                v_plane[g, h] = keep.tile([P, BANK], U8, name="v_plane_%d_%d" % (g, h), align_bytes=64)
+        bias = keep.tile([P, C], F32, name="bias")
+        m_cols = keep.tile([P, GROUPS, PACK], BF16, name="m_cols")
+        r_cols = keep.tile([P, CHUNKS], F32, name="r_cols")
+
+        def spread_bias():
+            ident_bf16 = keep.tile([P, P], BF16, name="ident_bf16")
+            nc.vector.tensor_copy(out=ident_bf16[:], in_=ident[:])
+            bank = psum.tile([P, PACK, P], BF16, name="bias_bank", tag="acc_0_0", bufs=1)
+            for j in range(PACK):
+                nc.tensor.transpose(bank[:, j, :], b_cols[:, j : j + 1].to_broadcast([P, P]), ident_bf16[:])
+            nc.scalar.activation(
+                out=bias[:].rearrange("p (n j) -> p n j", j=PACK), in_=bank[:].rearrange("p j n -> p n j"), func=ACT.Copy
+            )
+
+        def transpose_m_and_r():
+            r_rows = keep.tile([P, P], F32, name="r_rows")
+            nc.scalar.activation(out=r_rows[:], in_=mr_rows[:, PASS : PASS + P], func=ACT.Copy)
+            m_words = mr_rows[:, 0:PASS].bitcast(F32)
+            bank = psum.tile([P, 3, P], F32, name="mr_bank", tag="acc_0_1", bufs=1)
+            for e in range(2):
+                nc.tensor.transpose(bank[:, e, :], m_words[:, e : 2 * P : 2], ident[:])
+            nc.tensor.transpose(bank[:, 2, :], r_rows[:], ident[:])
+            return bank
+
+        def copy_m_and_r(bank):
+            nc.scalar.copy(
+                out=m_cols[:].rearrange("p g t -> p (g t)").bitcast(F32).rearrange("p (g e) -> p g e", e=2),
+                in_=bank[:, 0:2, 0:GROUPS].rearrange("p e g -> p g e"),
+            )
+            nc.scalar.copy(out=r_cols[:], in_=bank[:, 2, 0:CHUNKS])
 
         def transpose_x(u):
             words = x_sb[u].bitcast(F32)
-            if u in (2, 5):
-                xt_bank[u] = psum.tile([P, K_PASSES, 2, P], F32, name="xt_bank", tag="acc_1_0", bufs=1)
-            else:
-                xt_bank[u] = psum.tile([P, K_PASSES, 2, P], F32, name="xt_bank", tag="xt", bufs=2)
+            xt_bank[u] = psum.tile([P, K_PASSES, 2, P], F32, name="xt_bank", tag="xt", bufs=2)
             for h in range(K_PASSES):
                 for e in range(2):
-                    nc.tensor.transpose(xt_bank[u][:, h, e, :], words[:, 256 * h + e : 256 * (h + 1) : 2], ident[:])
+                    nc.tensor.transpose(xt_bank[u][:, h, e, :], words[:, 2 * P * h + e : 2 * P * (h + 1) : 2], ident[:])
 
         def copy_x(u):
-            xt_sb[u] = work.tile([P, K_PASSES * P * PACK], BF16, name="xt_sb", align_bytes=64)
+            xt_sb[u] = work.tile([P, K], BF16, name="xt_sb", align_bytes=64)
             nc.scalar.copy(
                 out=xt_sb[u][:].bitcast(F32).rearrange("p (h s e) -> p h s e", h=K_PASSES, e=2),
                 in_=xt_bank[u][:].rearrange("p h e s -> p h s e"),
@@ -122,7 +147,7 @@ def tile_scaled_cluster_sums_s9_kernel(tc, x, w_words, w_scales, b, m, v, r, out
             nc.vector.quantize_mx(out=x_codes[u][:].bitcast(E4M3), scales=x_plane[u][:], in_=xt_sb[u][:])
 
         def logits(u):
-            z_bank[u] = psum.tile([P, BANK], F32, name="z_bank", tag="z", bufs=2)
+            z_bank[u] = psum.tile([P, C], F32, name="z_bank", tag="z", bufs=2)
             for h in range(K_PASSES):
                 nc.tensor.matmul_mx(
                     out=z_bank[u][:],
@@ -134,18 +159,8 @@ def tile_scaled_cluster_sums_s9_kernel(tc, x, w_words, w_scales, b, m, v, r, out
                     stop=(h == K_PASSES - 1),
                 )
 
-        def turn_m_and_r():
-            r_rows = keep.tile([P, P], F32, name="r_rows")
-            nc.scalar.activation(out=r_rows[:], in_=rows_mr[:, GROUP : GROUP + P], func=ACT.Copy)
-            m_words = rows_mr[:, 0:GROUP].bitcast(F32)
-            bank = psum.tile([P, 3, P], F32, name="mr_bank", tag="acc_0_1", bufs=1)
-            for e in range(2):
-                nc.tensor.transpose(bank[:, e, :], m_words[:, e : 2 * P : 2], ident[:])
-            nc.tensor.transpose(bank[:, 2, :], r_rows[:], ident[:])
-            return bank
-
         def add_bias(u):
-            zb_sb[u] = work.tile([P, BANK], F32, name="zb_sb")
+            zb_sb[u] = work.tile([P, C], F32, name="zb_sb")
             nc.vector.tensor_tensor(out=zb_sb[u][:], in0=z_bank[u][:], in1=bias[:], op=ALU.add)
 
         def exp_scores(u):
@@ -154,166 +169,148 @@ def tile_scaled_cluster_sums_s9_kernel(tc, x, w_words, w_scales, b, m, v, r, out
             if t % 2 == 1:
                 nc.sync.dma_start(out=score_rows[g, :, t - 1 : t + 1, :], in_=scores[g][:, t - 1 : t + 1, :])
 
-        def weigh(n):
-            g, j = divmod(n, CHUNKS)
-            a_sb[n] = work.tile([P, P * PACK], BF16, name="a_sb", align_bytes=64)
+        def weigh(g, j):
+            a_sb[g, j] = work.tile([P, P * PACK], BF16, name="a_sb", align_bytes=64)
             nc.vector.tensor_tensor(
-                out=a_sb[n][:].rearrange("p (c i t) -> p c t i", i=2, t=PACK),
+                out=a_sb[g, j][:].rearrange("p (c i t) -> p c t i", i=2, t=PACK),
                 in0=scores[g][:, :, j * P : (j + 1) * P].rearrange("p t (c i) -> p c t i", i=2),
                 in1=m_cols[:, g, :].unsqueeze(1).unsqueeze(3).broadcast_to([P, P // 2, PACK, 2]),
                 op=ALU.mult,
             )
 
-        def quantize_a(n):
-            a_codes[n] = keep.tile([P, P], U32, name="a_codes_%d" % n, align_bytes=64)
-            a_plane[n] = keep.tile([P, P], U8, name="a_plane_%d" % n, align_bytes=64)
-            nc.vector.quantize_mx(out=a_codes[n][:].bitcast(E5M2), scales=a_plane[n][:], in_=a_sb[n][:])
+        def quantize_a(g, j):
+            a_codes[g, j] = keep.tile([P, P], U32, name="a_codes_%d_%d" % (g, j), align_bytes=64)
+            a_plane[g, j] = keep.tile([P, P], U8, name="a_plane_%d_%d" % (g, j), align_bytes=64)
+            nc.vector.quantize_mx(out=a_codes[g, j][:].bitcast(E5M2), scales=a_plane[g, j][:], in_=a_sb[g, j][:])
 
-        def interleave_v(k, copy, c0, width):
-            if c0 == 0:
-                vi_sb[k] = work.tile([P, PIECE * PACK], BF16, name="vi_sb", align_bytes=64, bufs=6)
+        def interleave_v(k, copy, c0=0, width=PIECE):
+            g, h = divmod(k // 2, HALVES)
+            if k % 2 == 0 and c0 == 0:
+                vi_sb[g, h] = work.tile([P, BANK * PACK], BF16, name="vi_sb", align_bytes=64)
+            d0 = (k % 2) * PIECE + c0
             copy(
-                out=vi_sb[k][:, c0 * PACK : (c0 + width) * PACK].rearrange("p (c i t) -> p c t i", i=4, t=PACK),
+                out=vi_sb[g, h][:, d0 * PACK : (d0 + width) * PACK].rearrange("p (c i t) -> p c t i", i=4, t=PACK),
                 in_=v_sb[k][:, :, c0 : c0 + width].rearrange("p t (c i) -> p c t i", i=4),
             )
 
-        def quantize_v(k):
-            g, q = divmod(k, PIECES)
-            h, cols = q // 2, slice((q % 2) * PIECE, (q % 2 + 1) * PIECE)
-            nc.vector.quantize_mx(out=v_codes[g, h][:, cols].bitcast(E4M3), scales=v_plane[g, h][:, cols], in_=vi_sb[k][:])
+        def quantize_v(g, h):
+            v_codes[g, h] = keep.tile([P, BANK], U32, name="v_codes_%d_%d" % (g, h), align_bytes=64)
+            v_plane[g, h] = keep.tile([P, BANK], U8, name="v_plane_%d_%d" % (g, h), align_bytes=64)
+            nc.vector.quantize_mx(out=v_codes[g, h][:].bitcast(E4M3), scales=v_plane[g, h][:], in_=vi_sb[g, h][:])
 
         def sums(g, j, h):
             if g == 0:
-                tag = ["acc_0_%d" % h, "acc_1_%d" % h, "xt", "z"][j]
-                acc[j, h] = psum.tile([P, BANK], F32, name="acc", tag=tag, bufs=1 if j < 2 else 2)
-            n = CHUNKS * g + j
+                tag, bufs = [("acc_0_%d" % h, 1), ("acc_1_%d" % h, 1), ("xt", 2), ("z", 2)][j]
+                acc[j, h] = psum.tile([P, BANK], F32, name="acc", tag=tag, bufs=bufs)
             nc.tensor.matmul_mx(
                 out=acc[j, h][:],
-                lhsT=a_codes[n][:].bitcast(E5M2),
-                lhsT_scale=a_plane[n][:],
+                lhsT=a_codes[g, j][:].bitcast(E5M2),
+                lhsT_scale=a_plane[g, j][:],
                 rhs=v_codes[g, h][:].bitcast(E4M3),
                 rhs_scale=v_plane[g, h][:],
                 start=(g == 0),
-                stop=(g == LAST),
+                stop=(g == LAST_GROUP),
             )
 
-        def centres(j, h, on_vector, parts=1):
+        def centres(j, h, on_vector=False, parts=1):
             width = BANK // parts
             for i in range(parts):
                 cen = keep.tile([P, width], F32, name="cen_%d_%d_%d" % (j, h, i))
                 src = acc[j, h][:, i * width : (i + 1) * width]
                 if on_vector:
-                    nc.vector.tensor_scalar(out=cen[:], in0=src, scalar1=r_f32[:, j : j + 1], scalar2=None, op0=ALU.mult)
+                    nc.vector.tensor_scalar(out=cen[:], in0=src, scalar1=r_cols[:, j : j + 1], scalar2=None, op0=ALU.mult)
                 else:
-                    nc.scalar.activation(out=cen[:], in_=src, func=ACT.Copy, scale=r_f32[:, j : j + 1])
+                    nc.scalar.activation(out=cen[:], in_=src, func=ACT.Copy, scale=r_cols[:, j : j + 1])
                 d0 = h * BANK + i * width
                 nc.sync.dma_start(out=out_1[j * P : (j + 1) * P, d0 : d0 + width], in_=cen[:])
 
-        b_f32 = keep.tile([P, PACK], F32, name="b_f32")
-        nc.scalar.activation(out=b_f32[:], in_=b_cols[:], func=ACT.Copy)
+        weigh_at = {PACK * g + 5 + j: (g, j) for g in range(LAST_GROUP) for j in range(LAST_CHUNK)}
+        vector_v_at = {0: [0, 1], 2: [2], 3: [3], 4: [4], 8: [8], 12: [10]}
+        scalar_v = [5, 6, 7, 9, 11, 12, 13]
+        scalar_v_at = {s: [s - 4] for s in range(4, 14)}
+        scalar_v_at[14] = [10, 11]
+        scalar_v_at[15] = [12, 13]
+        quantize_v_at = {1: (0, 0), 4: (0, 1), 6: (1, 0), 10: (1, 1), 12: (2, 0), 14: (2, 1)}
+        sums_at = {7: [(0, 0, 0)], 8: [(0, 0, 1)], 9: [(0, 1, 0)], 10: [(0, 1, 1)],
+                   11: [(1, 0, 0)], 12: [(1, 0, 1)], 13: [(1, 1, 0)], 14: [(1, 1, 1), (0, 2, 0), (1, 2, 0)],
+                   15: [(2, 0, 0), (0, 2, 1), (1, 2, 1), (2, 0, 1)]}
+
+        spread_bias()
         transpose_x(0)
-        bias_bank = psum.tile([P, PACK, P], F32, name="bias_bank", tag="acc_0_0", bufs=1)
-        for j in range(PACK):
-            nc.tensor.transpose(bias_bank[:, j, :], b_f32[:, j : j + 1].to_broadcast([P, P]), ident[:])
         transpose_x(1)
         copy_x(0)
-        bias = keep.tile([P, C], F32, name="bias")
-        nc.scalar.copy(out=bias[:].rearrange("p (n j) -> p n j", j=PACK), in_=bias_bank[:].rearrange("p j n -> p n j"))
-        interleave_v(0, nc.vector.tensor_copy, 0, PIECE)
-        quantize_v(0)
-        r_f32 = keep.tile([P, CHUNKS], F32, name="r_f32")
-        m_cols = keep.tile([P, GROUPS, PACK], BF16, name="m_cols")
-
-        weigh_at = {PACK * g + 5 + j: CHUNKS * g + j for g in range(LAST) for j in range(3)}
-        vector_v_at = {0: [1], 2: [2], 3: [3], 4: [4], 8: [8], 12: [11]}
-        scalar_v = [5, 6, 7, 9, 10, 12, 13]
-        scalar_at = {14: [10, 11], 15: [12, 13]}
-        for s in range(4, TILES - 2):
-            scalar_at[s] = [s - 4]
-        sums_at = {6: [(0, 0, 0)], 7: [(0, 0, 1)], 8: [(0, 1, 0)], 9: [(0, 1, 1)],
-                   10: [(1, 0, 0)], 11: [(1, 0, 1)], 12: [(1, 1, 0)], 13: [(1, 1, 1), (0, 2, 0), (1, 2, 0)],
-                   14: [(2, 0, 0), (0, 2, 1), (1, 2, 1), (2, 0, 1)],
-                   15: [(2, 1, 0), (2, 1, 1)]}
-        weighed, interleaved = None, []
+        quantize_x(0)
         for s in range(TILES):
             if s + 1 < TILES:
                 copy_x(s + 1)
-            quantize_x(s)
-            logits(s)
-            if s == 0:
-                transpose_x(2)
-            if s < 5:
-                transpose_x(s + 3)
-            elif s > 5 and s + 2 < TILES:
+            if s != 1 and s + 2 < TILES:
                 transpose_x(s + 2)
-            if s == 3:
-                mr_bank = turn_m_and_r()
-            if s == 4:
-                nc.scalar.copy(out=m_cols[:].rearrange("p g t -> p (g t)").bitcast(F32).rearrange("p (g e) -> p g e", e=2),
-                               in_=mr_bank[:, 0:2, 0:GROUPS].rearrange("p e g -> p g e"))
-                nc.scalar.copy(out=r_f32[:], in_=mr_bank[:, 2, 0:CHUNKS])
-            if s >= 1:
-                add_bias(s - 1)
-            if weighed is not None:
-                quantize_a(weighed)
-            weighed = weigh_at.get(s)
-            if weighed is not None:
-                weigh(weighed)
-            for k in vector_v_at.get(s, []):
-                interleave_v(k, nc.vector.tensor_copy, 0, PIECE)
-            for k in interleaved:
-                quantize_v(k)
-            interleaved = list(vector_v_at.get(s, []))
-            for n in scalar_at.get(s, []):
-                i, half = divmod(n, 2)
-                interleave_v(scalar_v[i], nc.scalar.copy, half * PIECE // 2, PIECE // 2)
-                if half == 1:
-                    interleaved.append(scalar_v[i])
-            if s >= 1:
-                exp_scores(s - 1)
             for g, j, h in sums_at.get(s, []):
                 sums(g, j, h)
+            if s != 1:
+                quantize_x(max(s, 1))
+            logits(s)
+            if s == 1:
+                transpose_x(3)
+            if s == 3:
+                mr_bank = transpose_m_and_r()
+            if s == 4:
+                copy_m_and_r(mr_bank)
+            if s >= 1:
+                add_bias(s - 1)
+            if s - 1 in weigh_at:
+                quantize_a(*weigh_at[s - 1])
+            if s in weigh_at:
+                weigh(*weigh_at[s])
+            for k in vector_v_at.get(s, []):
+                interleave_v(k, nc.vector.tensor_copy)
+            if s in quantize_v_at:
+                quantize_v(*quantize_v_at[s])
+            for n in scalar_v_at.get(s, []):
+                interleave_v(scalar_v[n // 2], nc.scalar.copy, (n % 2) * PIECE // 2, PIECE // 2)
+            if s >= 1:
+                exp_scores(s - 1)
 
+        for h in range(HALVES):
+            sums(2, 1, h)
         add_bias(TILES - 1)
         exp_scores(TILES - 1)
-        interleave_v(14, nc.scalar.copy, 0, PIECE)
-        interleave_v(15, nc.scalar.copy, 0, PIECE)
-        quantize_a(weighed)
+        interleave_v(14, nc.scalar.copy)
+        interleave_v(15, nc.scalar.copy)
+        quantize_a(2, 2)
         for h in range(HALVES):
-            sums(LAST - 1, 2, h)
-        for k in interleaved:
-            quantize_v(k)
-        weigh(3)
-        weigh(12)
-        quantize_a(3)
-        sums(0, 3, 0)
-        sums(0, 3, 1)
-        weigh(13)
-        quantize_a(12)
+            sums(2, 2, h)
+        quantize_v(3, 0)
+        weigh(0, 3)
+        weigh(3, 0)
+        quantize_a(0, 3)
+        for h in range(HALVES):
+            sums(0, 3, h)
+        weigh(3, 1)
+        quantize_a(3, 0)
         sums(3, 0, 0)
-        weigh(14)
-        quantize_a(13)
+        weigh(3, 2)
+        quantize_a(3, 1)
         sums(3, 1, 0)
-        quantize_v(14)
-        quantize_a(14)
+        quantize_v(3, 1)
+        quantize_a(3, 2)
         sums(3, 2, 0)
-        quantize_v(15)
-        for j in range(3):
+        for j in range(LAST_CHUNK):
             sums(3, j, 1)
         for h in range(HALVES):
-            for j in range(3):
-                centres(j, h, False)
-        weigh(7)
-        weigh(11)
-        quantize_a(7)
-        sums(1, 3, 0)
-        sums(1, 3, 1)
-        weigh(15)
-        quantize_a(11)
+            for j in range(LAST_CHUNK):
+                centres(j, h)
+        weigh(1, 3)
+        weigh(2, 3)
+        quantize_a(1, 3)
+        for h in range(HALVES):
+            sums(1, 3, h)
+        weigh(3, 3)
+        quantize_a(2, 3)
         sums(2, 3, 0)
-        quantize_a(15)
+        quantize_a(3, 3)
         sums(3, 3, 0)
         sums(2, 3, 1)
         sums(3, 3, 1)
-        centres(3, 0, True, 2)
-        centres(3, 1, False, 2)
+        centres(3, 0, on_vector=True, parts=2)
+        centres(3, 1, parts=2)

from contextlib import ExitStack

import concourse.mybir as mybir
from concourse.masks import make_identity

M, K, C, D = 2048, 1024, 512, 1024
FLOPS = 2 * M * K * C + 2 * M * C * D

F32 = mybir.dt.float32
BF16 = mybir.dt.bfloat16
I32 = mybir.dt.int32
U32 = mybir.dt.uint32
U8 = mybir.dt.uint8
E4M3 = mybir.dt.float8_e4m3fn_x4
E5M2 = mybir.dt.float8_e5m2_x4
E2M1 = mybir.dt.float4_e2m1fn_x4
ACT = mybir.ActivationFunctionType
ALU = mybir.AluOpType

P = 128
PACK = 4
PASS = P * PACK
K_PASSES = K // PASS
GROUPS = M // PASS
TILES = GROUPS * PACK
CHUNKS = C // P
BANK = 512
HALVES = D // BANK
PIECE = BANK // 2
PIECES = D // PIECE
LAST_GROUP = GROUPS - 1
LAST_CHUNK = CHUNKS - 1


def tile_scaled_cluster_sums_s9_kernel(tc, x, w_words, w_scales, b, m, v, r, out_0, out_1):
    nc = tc.nc
    x_rows = x.rearrange("(g p t) k -> g p t k", p=P, t=PACK)
    v_rows = v.rearrange("(g p t) d -> g p t d", p=P, t=PACK)
    score_rows = out_0.rearrange("(g p t) c -> g p t c", p=P, t=PACK)

    with ExitStack() as ctx:
        keep = ctx.enter_context(tc.tile_pool(name="keep", bufs=1))
        work = ctx.enter_context(tc.tile_pool(name="work", bufs=3))
        psum = ctx.enter_context(tc.psum_pool(name="psum", bufs=1))
        ctx.enter_context(tc.manual_schedule())

        ident = keep.tile([P, P], F32, name="ident")
        make_identity(nc, ident[:])
        mr_rows = keep.tile([P, PASS + P], BF16, name="mr_rows")
        nc.gpsimd.memset(mr_rows[:].bitcast(I32), 0)
        w_plane = keep.tile([P, K_PASSES, C], U8, name="w_plane", align_bytes=64)
        nc.vector.memset(w_plane[:].rearrange("p h c -> p (h c)").bitcast(I32), 0)

        x_sb, v_sb = {}, {}

        def load_x(u, count):
            g, t = divmod(u, PACK)
            rows = keep.tile([P, count, K], BF16, name="x_%d" % u)
            nc.sync.dma_start(out=rows[:], in_=x_rows[g, :, t : t + count, :])
            for i in range(count):
                x_sb[u + i] = rows[:, i, :]

        def load_v(k, count):
            g, q = divmod(k, PIECES)
            cols = keep.tile([P, PACK, count * PIECE], BF16, name="v_%d" % k)
            nc.sync.dma_start(out=cols[:], in_=v_rows[g, :, :, q * PIECE : (q + count) * PIECE])
            for i in range(count):
                v_sb[k + i] = cols[:, :, i * PIECE : (i + 1) * PIECE]

        b_cols = keep.tile([P, PACK], BF16, name="b_cols")
        nc.sync.dma_start(out=b_cols[:], in_=b.rearrange("(p j) -> p j", j=PACK))
        load_x(0, 1)
        load_x(1, 2)
        w_codes = keep.tile([P, K_PASSES, 2 * C], U8, name="w_codes", align_bytes=64)
        nc.sync.dma_start(out=w_codes[:].bitcast(I32), in_=w_words.rearrange("h p n -> p h n").bitcast(I32))
        for quad in range(4):
            nc.sync.dma_start(
                out=w_plane[32 * quad : 32 * quad + 4, :, :].bitcast(I32),
                in_=w_scales[:, 4 * quad : 4 * quad + 4, :].rearrange("h q c -> q h c").bitcast(I32),
            )
        load_v(0, 2)
        load_x(3, 1)
        load_x(4, 2)
        load_v(2, 2)
        load_x(6, 2)
        nc.sync.dma_start(out=mr_rows[0:GROUPS, 0:PASS], in_=m.rearrange("(g s) -> g s", g=GROUPS))
        nc.sync.dma_start(out=mr_rows[0:CHUNKS, PASS : PASS + P], in_=r.rearrange("(j c) -> j c", j=CHUNKS))
        load_v(4, 2)
        load_x(8, PACK)
        load_v(6, 2)
        load_v(8, PIECES)
        load_x(12, PACK)
        load_v(12, PIECES)

        xt_bank, xt_sb, x_codes, x_plane = {}, {}, {}, {}
        z_bank, zb_sb, a_sb, a_codes, a_plane = {}, {}, {}, {}, {}
        vi_sb, v_codes, v_plane, acc = {}, {}, {}, {}
        scores = [keep.tile([P, PACK, C], F32, name="scores_%d" % g) for g in range(GROUPS)]
        bias = keep.tile([P, C], F32, name="bias")
        m_cols = keep.tile([P, GROUPS, PACK], BF16, name="m_cols")
        r_cols = keep.tile([P, CHUNKS], F32, name="r_cols")

        def spread_bias():
            ident_bf16 = keep.tile([P, P], BF16, name="ident_bf16")
            nc.vector.tensor_copy(out=ident_bf16[:], in_=ident[:])
            bank = psum.tile([P, PACK, P], BF16, name="bias_bank", tag="acc_0_0", bufs=1)
            for j in range(PACK):
                nc.tensor.transpose(bank[:, j, :], b_cols[:, j : j + 1].to_broadcast([P, P]), ident_bf16[:])
            nc.scalar.activation(
                out=bias[:].rearrange("p (n j) -> p n j", j=PACK), in_=bank[:].rearrange("p j n -> p n j"), func=ACT.Copy
            )

        def transpose_m_and_r():
            r_rows = keep.tile([P, P], F32, name="r_rows")
            nc.scalar.activation(out=r_rows[:], in_=mr_rows[:, PASS : PASS + P], func=ACT.Copy)
            m_words = mr_rows[:, 0:PASS].bitcast(F32)
            bank = psum.tile([P, 3, P], F32, name="mr_bank", tag="acc_0_1", bufs=1)
            for e in range(2):
                nc.tensor.transpose(bank[:, e, :], m_words[:, e : 2 * P : 2], ident[:])
            nc.tensor.transpose(bank[:, 2, :], r_rows[:], ident[:])
            return bank

        def copy_m_and_r(bank):
            nc.scalar.copy(
                out=m_cols[:].rearrange("p g t -> p (g t)").bitcast(F32).rearrange("p (g e) -> p g e", e=2),
                in_=bank[:, 0:2, 0:GROUPS].rearrange("p e g -> p g e"),
            )
            nc.scalar.copy(out=r_cols[:], in_=bank[:, 2, 0:CHUNKS])

        def transpose_x(u):
            words = x_sb[u].bitcast(F32)
            xt_bank[u] = psum.tile([P, K_PASSES, 2, P], F32, name="xt_bank", tag="xt", bufs=2)
            for h in range(K_PASSES):
                for e in range(2):
                    nc.tensor.transpose(xt_bank[u][:, h, e, :], words[:, 2 * P * h + e : 2 * P * (h + 1) : 2], ident[:])

        def copy_x(u):
            xt_sb[u] = work.tile([P, K], BF16, name="xt_sb", align_bytes=64)
            nc.scalar.copy(
                out=xt_sb[u][:].bitcast(F32).rearrange("p (h s e) -> p h s e", h=K_PASSES, e=2),
                in_=xt_bank[u][:].rearrange("p h e s -> p h s e"),
            )

        def quantize_x(u):
            x_codes[u] = keep.tile([P, K_PASSES * P], U32, name="x_codes_%d" % u, align_bytes=64)
            x_plane[u] = keep.tile([P, K_PASSES * P], U8, name="x_plane_%d" % u, align_bytes=64)
            nc.vector.quantize_mx(out=x_codes[u][:].bitcast(E4M3), scales=x_plane[u][:], in_=xt_sb[u][:])

        def logits(u):
            z_bank[u] = psum.tile([P, C], F32, name="z_bank", tag="z", bufs=2)
            for h in range(K_PASSES):
                nc.tensor.matmul_mx(
                    out=z_bank[u][:],
                    lhsT=x_codes[u][:, h * P : (h + 1) * P].bitcast(E4M3),
                    lhsT_scale=x_plane[u][:, h * P : (h + 1) * P],
                    rhs=w_codes[:, h, :].bitcast(E2M1),
                    rhs_scale=w_plane[:, h, :],
                    start=(h == 0),
                    stop=(h == K_PASSES - 1),
                )

        def add_bias(u):
            zb_sb[u] = work.tile([P, C], F32, name="zb_sb")
            nc.vector.tensor_tensor(out=zb_sb[u][:], in0=z_bank[u][:], in1=bias[:], op=ALU.add)

        def exp_scores(u):
            g, t = divmod(u, PACK)
            nc.scalar.activation(out=scores[g][:, t, :], in_=zb_sb[u][:], func=ACT.Exp)
            if t % 2 == 1:
                nc.sync.dma_start(out=score_rows[g, :, t - 1 : t + 1, :], in_=scores[g][:, t - 1 : t + 1, :])

        def weigh(g, j):
            a_sb[g, j] = work.tile([P, P * PACK], BF16, name="a_sb", align_bytes=64)
            nc.vector.tensor_tensor(
                out=a_sb[g, j][:].rearrange("p (c i t) -> p c t i", i=2, t=PACK),
                in0=scores[g][:, :, j * P : (j + 1) * P].rearrange("p t (c i) -> p c t i", i=2),
                in1=m_cols[:, g, :].unsqueeze(1).unsqueeze(3).broadcast_to([P, P // 2, PACK, 2]),
                op=ALU.mult,
            )

        def quantize_a(g, j):
            a_codes[g, j] = keep.tile([P, P], U32, name="a_codes_%d_%d" % (g, j), align_bytes=64)
            a_plane[g, j] = keep.tile([P, P], U8, name="a_plane_%d_%d" % (g, j), align_bytes=64)
            nc.vector.quantize_mx(out=a_codes[g, j][:].bitcast(E5M2), scales=a_plane[g, j][:], in_=a_sb[g, j][:])

        def interleave_v(k, copy, c0=0, width=PIECE):
            g, h = divmod(k // 2, HALVES)
            if k % 2 == 0 and c0 == 0:
                vi_sb[g, h] = work.tile([P, BANK * PACK], BF16, name="vi_sb", align_bytes=64)
            d0 = (k % 2) * PIECE + c0
            copy(
                out=vi_sb[g, h][:, d0 * PACK : (d0 + width) * PACK].rearrange("p (c i t) -> p c t i", i=4, t=PACK),
                in_=v_sb[k][:, :, c0 : c0 + width].rearrange("p t (c i) -> p c t i", i=4),
            )

        def quantize_v(g, h):
            v_codes[g, h] = keep.tile([P, BANK], U32, name="v_codes_%d_%d" % (g, h), align_bytes=64)
            v_plane[g, h] = keep.tile([P, BANK], U8, name="v_plane_%d_%d" % (g, h), align_bytes=64)
            nc.vector.quantize_mx(out=v_codes[g, h][:].bitcast(E4M3), scales=v_plane[g, h][:], in_=vi_sb[g, h][:])

        def sums(g, j, h):
            if g == 0:
                tag, bufs = [("acc_0_%d" % h, 1), ("acc_1_%d" % h, 1), ("xt", 2), ("z", 2)][j]
                acc[j, h] = psum.tile([P, BANK], F32, name="acc", tag=tag, bufs=bufs)
            nc.tensor.matmul_mx(
                out=acc[j, h][:],
                lhsT=a_codes[g, j][:].bitcast(E5M2),
                lhsT_scale=a_plane[g, j][:],
                rhs=v_codes[g, h][:].bitcast(E4M3),
                rhs_scale=v_plane[g, h][:],
                start=(g == 0),
                stop=(g == LAST_GROUP),
            )

        def centres(j, h, on_vector=False, parts=1):
            width = BANK // parts
            for i in range(parts):
                cen = keep.tile([P, width], F32, name="cen_%d_%d_%d" % (j, h, i))
                src = acc[j, h][:, i * width : (i + 1) * width]
                if on_vector:
                    nc.vector.tensor_scalar(out=cen[:], in0=src, scalar1=r_cols[:, j : j + 1], scalar2=None, op0=ALU.mult)
                else:
                    nc.scalar.activation(out=cen[:], in_=src, func=ACT.Copy, scale=r_cols[:, j : j + 1])
                d0 = h * BANK + i * width
                nc.sync.dma_start(out=out_1[j * P : (j + 1) * P, d0 : d0 + width], in_=cen[:])

        weigh_at = {PACK * g + 5 + j: (g, j) for g in range(LAST_GROUP) for j in range(LAST_CHUNK)}
        vector_v_at = {0: [0, 1], 2: [2], 3: [3], 4: [4], 8: [8], 12: [10]}
        scalar_v = [5, 6, 7, 9, 11, 12, 13]
        scalar_v_at = {s: [s - 4] for s in range(4, 14)}
        scalar_v_at[14] = [10, 11]
        scalar_v_at[15] = [12, 13]
        quantize_v_at = {1: (0, 0), 4: (0, 1), 6: (1, 0), 10: (1, 1), 12: (2, 0), 14: (2, 1)}
        sums_at = {7: [(0, 0, 0)], 8: [(0, 0, 1)], 9: [(0, 1, 0)], 10: [(0, 1, 1)],
                   11: [(1, 0, 0)], 12: [(1, 0, 1)], 13: [(1, 1, 0)], 14: [(1, 1, 1), (0, 2, 0), (1, 2, 0)],
                   15: [(2, 0, 0), (0, 2, 1), (1, 2, 1), (2, 0, 1)]}

        spread_bias()
        transpose_x(0)
        transpose_x(1)
        copy_x(0)
        quantize_x(0)
        for s in range(TILES):
            if s + 1 < TILES:
                copy_x(s + 1)
            if s != 1 and s + 2 < TILES:
                transpose_x(s + 2)
            for g, j, h in sums_at.get(s, []):
                sums(g, j, h)
            if s != 1:
                quantize_x(max(s, 1))
            logits(s)
            if s == 1:
                transpose_x(3)
            if s == 3:
                mr_bank = transpose_m_and_r()
            if s == 4:
                copy_m_and_r(mr_bank)
            if s >= 1:
                add_bias(s - 1)
            if s - 1 in weigh_at:
                quantize_a(*weigh_at[s - 1])
            if s in weigh_at:
                weigh(*weigh_at[s])
            for k in vector_v_at.get(s, []):
                interleave_v(k, nc.vector.tensor_copy)
            if s in quantize_v_at:
                quantize_v(*quantize_v_at[s])
            for n in scalar_v_at.get(s, []):
                interleave_v(scalar_v[n // 2], nc.scalar.copy, (n % 2) * PIECE // 2, PIECE // 2)
            if s >= 1:
                exp_scores(s - 1)

        for h in range(HALVES):
            sums(2, 1, h)
        add_bias(TILES - 1)
        exp_scores(TILES - 1)
        interleave_v(14, nc.scalar.copy)
        interleave_v(15, nc.scalar.copy)
        quantize_a(2, 2)
        for h in range(HALVES):
            sums(2, 2, h)
        quantize_v(3, 0)
        weigh(0, 3)
        weigh(3, 0)
        quantize_a(0, 3)
        for h in range(HALVES):
            sums(0, 3, h)
        weigh(3, 1)
        quantize_a(3, 0)
        sums(3, 0, 0)
        weigh(3, 2)
        quantize_a(3, 1)
        sums(3, 1, 0)
        quantize_v(3, 1)
        quantize_a(3, 2)
        sums(3, 2, 0)
        for j in range(LAST_CHUNK):
            sums(3, j, 1)
        for h in range(HALVES):
            for j in range(LAST_CHUNK):
                centres(j, h)
        weigh(1, 3)
        weigh(2, 3)
        quantize_a(1, 3)
        for h in range(HALVES):
            sums(1, 3, h)
        weigh(3, 3)
        quantize_a(2, 3)
        sums(2, 3, 0)
        quantize_a(3, 3)
        sums(3, 3, 0)
        sums(2, 3, 1)
        sums(3, 3, 1)
        centres(3, 0, on_vector=True, parts=2)
        centres(3, 1, parts=2)
